import numpy as np
import ml_dtypes


def mxq(x, axis, fmt="e4m3"):
    dtype, down = {"e4m3": (ml_dtypes.float8_e4m3fn, 7), "e5m2": (ml_dtypes.float8_e5m2, 14)}[fmt]
    v = np.moveaxis(np.asarray(x, np.float32).astype(ml_dtypes.bfloat16).astype(np.float64), axis, -1)
    blocks = v.reshape(v.shape[:-1] + (-1, 32))
    amax = np.abs(blocks).max(-1, keepdims=True)
    byte = np.maximum(np.where(amax > 0, np.frexp(amax)[1] - 1 + 127, 0) - down, 1)
    scale = np.exp2(byte - 127.0)
    codes = (blocks / scale).astype(np.float32).astype(dtype).astype(np.float64)
    return np.moveaxis((codes * scale).reshape(v.shape), -1, axis)


WIDE = False


def mx_kscale(k):
    if not WIDE:
        return np.ones(k)
    levels = np.array([10, -10, 5, -5, 0])
    if k % 512:
        return np.exp2(np.random.permutation(np.resize(levels, k // 32))).repeat(32)
    a = np.empty((k // 512, 16))
    for p in range(k // 512):
        a[p, :8] = np.random.permutation(np.resize(levels, 8))
        for g in range(8):
            far = levels[np.abs(levels - a[p, g]) >= 10]
            a[p, g + 8] = far[np.random.randint(len(far))]
    return np.exp2(a.ravel()).repeat(32)


def f64(x):
    return np.asarray(x).astype(np.float64)


def striped(idx):
    return np.tile(idx.reshape(-1, 16).T, (8, 1)).astype(np.uint16)


def unstriped(offs):
    return offs[:16].T.reshape(-1).astype(np.int64)


def pack_weight(w):
    k, n = w.shape
    w = f64(np.asarray(w, np.float32).astype(ml_dtypes.bfloat16)).reshape(k // 32, 32, n)
    amax = np.abs(w).max(1)
    byte = np.clip(np.where(amax > 0, np.frexp(amax)[1] - 1 + 127 - 7, 1), 1, 254)
    scaled = (w * np.exp2(127.0 - byte)[:, None, :]).reshape(k, n).astype(np.float32)
    words = np.ascontiguousarray(scaled.reshape(k // 512, 128, 4, n).transpose(0, 1, 3, 2)).astype(ml_dtypes.float8_e4m3fn).view(np.uint8)
    return words, np.ascontiguousarray(byte.astype(np.uint8).reshape(k // 512, 16, n))


def unpack_weight(words, scales):
    g, p, n, _ = words.shape
    vals = np.ascontiguousarray(words).view(ml_dtypes.float8_e4m3fn).astype(np.float64) * np.repeat(np.exp2(scales.astype(np.float64) - 127.0), 8, axis=1)[..., None]
    return vals.transpose(0, 1, 3, 2).reshape(g * 512, n)


K, T, S, N = 1024, 1024, 512, 128


def setup_inputs():
    n = np.random.standard_normal
    s = mx_kscale(K)[:, None]
    packed_xT = pack_weight(n((K, T)) * s)
    return {
        "x_words": packed_xT[0],
        "x_scales": packed_xT[1],
        "w1": (n((K, N)) / np.sqrt(2 * K) / s).astype(np.float32),
        "w2": (n((K, N)) / np.sqrt(2 * K) / s).astype(np.float32),
        "offs": striped(np.random.permutation(T)[:S]),
    }


def reference(x_words, x_scales, w1, w2, offs):
    xq = unpack_weight(x_words, x_scales)[:, unstriped(offs)]
    y0 = mxq(f64(w1), 0, "e4m3").T @ xq
    y1 = mxq(f64(w2), 0, "e4m3").T @ xq
    return y0 + np.pad(y1, ((0, 0), (1, 0)))[:, :S]

@@ -1,0 +1,126 @@
+import concourse.mybir as mybir
+
+K, T, S, N = 1024, 1024, 512, 128
+FLOPS = 2 * 2 * K * N * S
+
+F32 = mybir.dt.float32
+BF16 = mybir.dt.bfloat16
+I32 = mybir.dt.int32
+U32 = mybir.dt.uint32
+U16 = mybir.dt.uint16
+U8 = mybir.dt.uint8
+FP8X4 = mybir.dt.float8_e4m3fn_x4
+
+P = 128
+PACK = 4
+K_PASS = P * PACK
+HALF = S // 2
+
+
+def tile_picked_listconv_none_p_kernel(tc, x_words, x_scales, w1, w2, offs, out):
+    nc = tc.nc
+    weights = (w1, w2)
+    with (
+        tc.tile_pool(name="sbuf", bufs=1) as pool,
+        tc.psum_pool(name="psum", bufs=1) as psum,
+    ):
+        offsets = pool.tile([P, S // 16], U16, name="offsets")
+        nc.sync.dma_start(offsets[:], offs)
+
+        scale_table = pool.tile([P, T], U8, name="scale_table", align_bytes=64)
+        nc.vector.memset(scale_table[:].bitcast(I32), 0)
+        for q in range(4):
+            nc.scalar.dma_start(
+                scale_table[32 * q : 32 * q + 8, :].bitcast(I32),
+                x_scales[:, 4 * q : 4 * q + 4, :].bitcast(I32),
+            )
+
+        zero = pool.tile([P, 1], F32, name="zero")
+        nc.vector.memset(zero[:], 0.0)
+        late = pool.tile([P, S], F32, name="late", align_bytes=64)
+        nc.scalar.copy(late[:, 0:1], zero[:])
+
+        word_table = {}
+        raw = {}
+
+        def load_words(z):
+            word_table[z] = pool.tile([P, T], I32, name="word_table%d" % z, align_bytes=64)
+            nc.sync.dma_start(word_table[z][:], x_words[z].rearrange("p n t -> p (n t)").bitcast(I32))
+
+        def load_weight(d, z):
+            raw[d, z] = pool.tile([P, PACK, N], F32, name="raw%d%d" % (d, z), align_bytes=64)
+            nc.sync.dma_start(
+                raw[d, z][:], weights[d][z * K_PASS : (z + 1) * K_PASS, :].rearrange("(p j) n -> p j n", j=PACK)
+            )
+
+        load_words(0)
+        load_weight(1, 0)
+        load_words(1)
+        load_weight(0, 0)
+        load_weight(1, 1)
+        load_weight(0, 1)
+
+        x_scale = pool.tile([P, S], U8, name="x_scale", align_bytes=64)
+        x_code = {}
+
+        def gather_words(z):
+            x_code[z] = pool.tile([P, S], U32, name="x_code%d" % z, align_bytes=64)
+            nc.vector.tensor_copy(x_code[z][:], word_table[z][:].bitcast(U32).indirect(offsets[:]))
+
+        grouped = {}
+        w_code = {}
+        w_scale = {}
+
+        def cast(d, z, copy):
+            grouped[d, z] = pool.tile([P, N, PACK], BF16, name="grouped%d%d" % (d, z), align_bytes=64)
+            copy(
+                grouped[d, z][:].rearrange("p (c i) t -> p c t i", i=4),
+                raw[d, z][:].rearrange("p t (c i) -> p c t i", i=4),
+            )
+
+        def quantise(d, z):
+            w_code[d, z] = pool.tile([P, N], U32, name="w_code%d%d" % (d, z), align_bytes=64)
+            w_scale[d, z] = pool.tile([P, N], U8, name="w_scale%d%d" % (d, z), align_bytes=64)
+            nc.vector.quantize_mx(
+                out=w_code[d, z][:].bitcast(FP8X4),
+                scales=w_scale[d, z][:],
+                in_=grouped[d, z][:].rearrange("p n t -> p (n t)"),
+            )
+
+        y1 = psum.tile([P, S], F32, name="y1")
+        y0 = [psum.tile([P, HALF], F32, name="y0_%d" % h) for h in range(2)]
+
+        def product(acc, d, z, cols):
+            nc.tensor.matmul_mx(
+                out=acc,
+                lhsT=w_code[d, z][:].bitcast(FP8X4),
+                lhsT_scale=w_scale[d, z][:],
+                rhs=x_code[z][:, cols].bitcast(FP8X4),
+                rhs_scale=x_scale[4 * z : P, cols],
+                start=(z == 0),
+                stop=(z == 1),
+            )
+
+        halves = [slice(h * HALF, (h + 1) * HALF) for h in range(2)]
+
+        nc.vector.tensor_copy(x_scale[:], scale_table[:].indirect(offsets[:]))
+        gather_words(0)
+        cast(1, 0, nc.scalar.copy)
+        quantise(1, 0)
+        product(y1[:], 1, 0, slice(0, S))
+        gather_words(1)
+        cast(0, 0, nc.scalar.copy)
+        quantise(0, 0)
+        for h in range(2):
+            product(y0[h][:], 0, 0, halves[h])
+        cast(1, 1, nc.scalar.copy)
+        quantise(1, 1)
+        product(y1[:], 1, 1, slice(0, S))
+        cast(0, 1, nc.vector.tensor_copy)
+        quantise(0, 1)
+        nc.scalar.copy(late[:, 1:S], y1[:, 0 : S - 1])
+        for h in range(2):
+            product(y0[h][:], 0, 1, halves[h])
+            result = pool.tile([P, HALF], F32, name="result%d" % h, align_bytes=64)
+            nc.vector.tensor_tensor(result[:], y0[h][:], late[:, halves[h]], mybir.AluOpType.add)
+            nc.sync.dma_start(out[:, halves[h]], result[:])

@@ -14,113 +14,111 @@ FP8X4 = mybir.dt.float8_e4m3fn_x4
 P = 128
 PACK = 4
 K_PASS = P * PACK
+PASSES = K // K_PASS
+QUADRANT = 32
+QUADRANT_BLOCKS = 4
+LIST_GROUP = 16
+ALIGN = 64
 HALF = S // 2
 
 
 def tile_picked_listconv_none_p_kernel(tc, x_words, x_scales, w1, w2, offs, out):
     nc = tc.nc
     weights = (w1, w2)
+    halves = [slice(0, HALF), slice(HALF, S)]
     with (
         tc.tile_pool(name="sbuf", bufs=1) as pool,
         tc.psum_pool(name="psum", bufs=1) as psum,
     ):
-        offsets = pool.tile([P, S // 16], U16, name="offsets")
+        offsets = pool.tile([P, S // LIST_GROUP], U16, name="offsets")
         nc.sync.dma_start(offsets[:], offs)
 
-        scale_table = pool.tile([P, T], U8, name="scale_table", align_bytes=64)
+        scale_table = pool.tile([P, T], U8, name="scale_table", align_bytes=ALIGN)
         nc.vector.memset(scale_table[:].bitcast(I32), 0)
-        for q in range(4):
-            nc.scalar.dma_start(
-                scale_table[32 * q : 32 * q + 8, :].bitcast(I32),
-                x_scales[:, 4 * q : 4 * q + 4, :].bitcast(I32),
+        for q in range(P // QUADRANT):
+            nc.sync.dma_start(
+                scale_table[QUADRANT * q : QUADRANT * q + PASSES * QUADRANT_BLOCKS, :].bitcast(I32),
+                x_scales[:, QUADRANT_BLOCKS * q : QUADRANT_BLOCKS * (q + 1), :].bitcast(I32),
             )
 
-        zero = pool.tile([P, 1], F32, name="zero")
+        zero = pool.tile([P, 1], F32, name="zero", align_bytes=ALIGN)
         nc.vector.memset(zero[:], 0.0)
-        late = pool.tile([P, S], F32, name="late", align_bytes=64)
-        nc.scalar.copy(late[:, 0:1], zero[:])
+        shifted = pool.tile([P, S], F32, name="shifted", align_bytes=ALIGN)
+        nc.scalar.copy(shifted[:, 0:1], zero[:])
 
         word_table = {}
-        raw = {}
+        w_rows = {}
 
         def load_words(z):
-            word_table[z] = pool.tile([P, T], I32, name="word_table%d" % z, align_bytes=64)
+            word_table[z] = pool.tile([P, T], I32, name="word_table%d" % z, align_bytes=ALIGN)
             nc.sync.dma_start(word_table[z][:], x_words[z].rearrange("p n t -> p (n t)").bitcast(I32))
 
-        def load_weight(d, z):
-            raw[d, z] = pool.tile([P, PACK, N], F32, name="raw%d%d" % (d, z), align_bytes=64)
-            nc.sync.dma_start(
-                raw[d, z][:], weights[d][z * K_PASS : (z + 1) * K_PASS, :].rearrange("(p j) n -> p j n", j=PACK)
-            )
+        def load_weight(tap, z, queue):
+            flat = pool.tile([P, PACK * N], F32, name="w_rows%d%d" % (tap, z), align_bytes=ALIGN)
+            w_rows[tap, z] = flat[:].rearrange("p (t m) -> p t m", t=PACK)
+            rows = weights[tap][z * K_PASS : (z + 1) * K_PASS, :]
+            queue.dma_start(flat[:], rows.rearrange("(p t) m -> p (t m)", t=PACK))
 
+        load_weight(1, 0, nc.scalar)
         load_words(0)
-        load_weight(1, 0)
+        load_weight(0, 0, nc.sync)
         load_words(1)
-        load_weight(0, 0)
-        load_weight(1, 1)
-        load_weight(0, 1)
+        load_weight(1, 1, nc.sync)
+        load_weight(0, 1, nc.sync)
 
-        x_scale = pool.tile([P, S], U8, name="x_scale", align_bytes=64)
+        x_planes = pool.tile([P, S], U8, name="x_planes", align_bytes=ALIGN)
         x_code = {}
 
         def gather_words(z):
-            x_code[z] = pool.tile([P, S], U32, name="x_code%d" % z, align_bytes=64)
+            x_code[z] = pool.tile([P, S], U32, name="x_code%d" % z, align_bytes=ALIGN)
             nc.vector.tensor_copy(x_code[z][:], word_table[z][:].bitcast(U32).indirect(offsets[:]))
 
-        grouped = {}
         w_code = {}
-        w_scale = {}
+        w_plane = {}
 
-        def cast(d, z, copy):
-            grouped[d, z] = pool.tile([P, N, PACK], BF16, name="grouped%d%d" % (d, z), align_bytes=64)
+        def quantise_weight(tap, z, copy):
+            grouped = pool.tile([P, N, PACK], BF16, name="grouped%d%d" % (tap, z), align_bytes=ALIGN)
             copy(
-                grouped[d, z][:].rearrange("p (c i) t -> p c t i", i=4),
-                raw[d, z][:].rearrange("p t (c i) -> p c t i", i=4),
+                grouped[:].rearrange("p (c i) t -> p c t i", i=4),
+                w_rows[tap, z].rearrange("p t (c i) -> p c t i", i=4),
             )
-
-        def quantise(d, z):
-            w_code[d, z] = pool.tile([P, N], U32, name="w_code%d%d" % (d, z), align_bytes=64)
-            w_scale[d, z] = pool.tile([P, N], U8, name="w_scale%d%d" % (d, z), align_bytes=64)
+            w_code[tap, z] = pool.tile([P, N], U32, name="w_code%d%d" % (tap, z), align_bytes=ALIGN)
+            w_plane[tap, z] = pool.tile([P, N], U8, name="w_plane%d%d" % (tap, z), align_bytes=ALIGN)
             nc.vector.quantize_mx(
-                out=w_code[d, z][:].bitcast(FP8X4),
-                scales=w_scale[d, z][:],
-                in_=grouped[d, z][:].rearrange("p n t -> p (n t)"),
+                out=w_code[tap, z][:].bitcast(FP8X4),
+                scales=w_plane[tap, z][:],
+                in_=grouped[:].rearrange("p m t -> p (m t)"),
             )
 
-        y1 = psum.tile([P, S], F32, name="y1")
-        y0 = [psum.tile([P, HALF], F32, name="y0_%d" % h) for h in range(2)]
+        acc = [[psum.tile([P, HALF], F32, name="acc%d%d" % (tap, h)) for h in range(2)] for tap in range(2)]
 
-        def product(acc, d, z, cols):
-            nc.tensor.matmul_mx(
-                out=acc,
-                lhsT=w_code[d, z][:].bitcast(FP8X4),
-                lhsT_scale=w_scale[d, z][:],
-                rhs=x_code[z][:, cols].bitcast(FP8X4),
-                rhs_scale=x_scale[4 * z : P, cols],
-                start=(z == 0),
-                stop=(z == 1),
-            )
+        def multiply(tap, z):
+            for h, cols in enumerate(halves):
+                nc.tensor.matmul_mx(
+                    out=acc[tap][h][:],
+                    lhsT=w_code[tap, z][:].bitcast(FP8X4),
+                    lhsT_scale=w_plane[tap, z][:],
+                    rhs=x_code[z][:, cols].bitcast(FP8X4),
+                    rhs_scale=x_planes[QUADRANT_BLOCKS * z : P, cols],
+                    start=(z == 0),
+                    stop=(z == PASSES - 1),
+                )
 
-        halves = [slice(h * HALF, (h + 1) * HALF) for h in range(2)]
-
-        nc.vector.tensor_copy(x_scale[:], scale_table[:].indirect(offsets[:]))
+        quantise_weight(1, 0, nc.vector.tensor_copy)
+        nc.vector.tensor_copy(x_planes[:], scale_table[:].indirect(offsets[:]))
         gather_words(0)
-        cast(1, 0, nc.scalar.copy)
-        quantise(1, 0)
-        product(y1[:], 1, 0, slice(0, S))
+        multiply(1, 0)
+        quantise_weight(0, 0, nc.scalar.copy)
+        multiply(0, 0)
         gather_words(1)
-        cast(0, 0, nc.scalar.copy)
-        quantise(0, 0)
-        for h in range(2):
-            product(y0[h][:], 0, 0, halves[h])
-        cast(1, 1, nc.scalar.copy)
-        quantise(1, 1)
-        product(y1[:], 1, 1, slice(0, S))
-        cast(0, 1, nc.vector.tensor_copy)
-        quantise(0, 1)
-        nc.scalar.copy(late[:, 1:S], y1[:, 0 : S - 1])
-        for h in range(2):
-            product(y0[h][:], 0, 1, halves[h])
-            result = pool.tile([P, HALF], F32, name="result%d" % h, align_bytes=64)
-            nc.vector.tensor_tensor(result[:], y0[h][:], late[:, halves[h]], mybir.AluOpType.add)
-            nc.sync.dma_start(out[:, halves[h]], result[:])
+        quantise_weight(1, 1, nc.scalar.copy)
+        quantise_weight(0, 1, nc.scalar.copy)
+        multiply(1, 1)
+
+        nc.scalar.copy(shifted[:, 1 : HALF + 1], acc[1][0][:])
+        nc.scalar.copy(shifted[:, HALF + 1 : S], acc[1][1][:, 0 : HALF - 1])
+        multiply(0, 1)
+        for h, cols in enumerate(halves):
+            result = pool.tile([P, HALF], F32, name="result%d" % h, align_bytes=ALIGN)
+            nc.vector.tensor_tensor(result[:], acc[0][h][:], shifted[:, cols], mybir.AluOpType.add)
+            nc.sync.dma_start(out[:, cols], result[:])

@@ -30,8 +30,22 @@ def tile_picked_listconv_none_p_kernel(tc, x_words, x_scales, w1, w2, offs, out)
         tc.tile_pool(name="sbuf", bufs=1) as pool,
         tc.psum_pool(name="psum", bufs=1) as psum,
     ):
+        word_table = {}
+        w_rows = {}
+
+        def load_words(z, queue):
+            word_table[z] = pool.tile([P, T], I32, name="word_table%d" % z, align_bytes=ALIGN)
+            queue.dma_start(word_table[z][:], x_words[z].rearrange("p n t -> p (n t)").bitcast(I32))
+
+        def load_weight(tap, z, queue):
+            flat = pool.tile([P, PACK * N], F32, name="w_rows%d%d" % (tap, z), align_bytes=ALIGN)
+            w_rows[tap, z] = flat[:].rearrange("p (t m) -> p t m", t=PACK)
+            rows = weights[tap][z * K_PASS : (z + 1) * K_PASS, :]
+            queue.dma_start(flat[:], rows.rearrange("(p t) m -> p (t m)", t=PACK))
+
         offsets = pool.tile([P, S // LIST_GROUP], U16, name="offsets")
         nc.sync.dma_start(offsets[:], offs)
+        load_words(0, nc.sync)
 
         scale_table = pool.tile([P, T], U8, name="scale_table", align_bytes=ALIGN)
         nc.vector.memset(scale_table[:].bitcast(I32), 0)
@@ -46,79 +60,110 @@ def tile_picked_listconv_none_p_kernel(tc, x_words, x_scales, w1, w2, offs, out)
         shifted = pool.tile([P, S], F32, name="shifted", align_bytes=ALIGN)
         nc.scalar.copy(shifted[:, 0:1], zero[:])
 
-        word_table = {}
-        w_rows = {}
-
-        def load_words(z):
-            word_table[z] = pool.tile([P, T], I32, name="word_table%d" % z, align_bytes=ALIGN)
-            nc.sync.dma_start(word_table[z][:], x_words[z].rearrange("p n t -> p (n t)").bitcast(I32))
-
-        def load_weight(tap, z, queue):
-            flat = pool.tile([P, PACK * N], F32, name="w_rows%d%d" % (tap, z), align_bytes=ALIGN)
-            w_rows[tap, z] = flat[:].rearrange("p (t m) -> p t m", t=PACK)
-            rows = weights[tap][z * K_PASS : (z + 1) * K_PASS, :]
-            queue.dma_start(flat[:], rows.rearrange("(p t) m -> p (t m)", t=PACK))
-
-        load_weight(1, 0, nc.scalar)
-        load_words(0)
+        load_weight(1, 0, nc.sync)
         load_weight(0, 0, nc.sync)
-        load_words(1)
+        load_words(1, nc.sync)
         load_weight(1, 1, nc.sync)
         load_weight(0, 1, nc.sync)
 
         x_planes = pool.tile([P, S], U8, name="x_planes", align_bytes=ALIGN)
-        x_code = {}
+        x_code = [pool.tile([P, S], U32, name="x_code%d" % z, align_bytes=ALIGN) for z in range(PASSES)]
 
-        def gather_words(z):
-            x_code[z] = pool.tile([P, S], U32, name="x_code%d" % z, align_bytes=ALIGN)
-            nc.vector.tensor_copy(x_code[z][:], word_table[z][:].bitcast(U32).indirect(offsets[:]))
+        def listed(cols):
+            return offsets[:, cols.start // LIST_GROUP : cols.stop // LIST_GROUP]
 
-        w_code = {}
-        w_plane = {}
+        def gather_scales(cols):
+            nc.vector.tensor_copy(x_planes[:, cols], scale_table[:].indirect(listed(cols)))
 
-        def quantise_weight(tap, z, copy):
-            grouped = pool.tile([P, N, PACK], BF16, name="grouped%d%d" % (tap, z), align_bytes=ALIGN)
+        def gather_words(z, cols):
+            nc.vector.tensor_copy(x_code[z][:, cols], word_table[z][:].bitcast(U32).indirect(listed(cols)))
+
+        grouped = [pool.tile([P, 2 * N * PACK], BF16, name="grouped%d" % z, align_bytes=ALIGN) for z in range(PASSES)]
+        w_code = [pool.tile([P, 2 * N], U32, name="w_code%d" % z, align_bytes=ALIGN) for z in range(PASSES)]
+        w_plane = [pool.tile([P, 2 * N], U8, name="w_plane%d" % z, align_bytes=ALIGN) for z in range(PASSES)]
+
+        def round_weight(tap, z, copy, first=0, last=N):
+            target = grouped[z][:, (tap * N + first) * PACK : (tap * N + last) * PACK]
             copy(
-                grouped[:].rearrange("p (c i) t -> p c t i", i=4),
-                w_rows[tap, z].rearrange("p t (c i) -> p c t i", i=4),
+                target.rearrange("p (c i t) -> p c t i", i=4, t=PACK),
+                w_rows[tap, z][:, :, first:last].rearrange("p t (c i) -> p c t i", i=4),
             )
-            w_code[tap, z] = pool.tile([P, N], U32, name="w_code%d%d" % (tap, z), align_bytes=ALIGN)
-            w_plane[tap, z] = pool.tile([P, N], U8, name="w_plane%d%d" % (tap, z), align_bytes=ALIGN)
+
+        def quantise(z, first, last):
             nc.vector.quantize_mx(
-                out=w_code[tap, z][:].bitcast(FP8X4),
-                scales=w_plane[tap, z][:],
-                in_=grouped[:].rearrange("p m t -> p (m t)"),
+                out=w_code[z][:, first:last].bitcast(FP8X4),
+                scales=w_plane[z][:, first:last],
+                in_=grouped[z][:, first * PACK : last * PACK],
             )
 
-        acc = [[psum.tile([P, HALF], F32, name="acc%d%d" % (tap, h)) for h in range(2)] for tap in range(2)]
+        pieces = [[slice(0, 128), slice(128, 256), slice(256, 384), slice(384, 512)], [slice(0, 128), slice(128, 256), slice(256, 384), slice(384, 512)]]
+        acc = [
+            [psum.tile([P, cols.stop - cols.start], F32, name="acc%d%d" % (tap, h)) for h, cols in enumerate(pieces[tap])]
+            for tap in range(2)
+        ]
 
-        def multiply(tap, z):
-            for h, cols in enumerate(halves):
-                nc.tensor.matmul_mx(
-                    out=acc[tap][h][:],
-                    lhsT=w_code[tap, z][:].bitcast(FP8X4),
-                    lhsT_scale=w_plane[tap, z][:],
-                    rhs=x_code[z][:, cols].bitcast(FP8X4),
-                    rhs_scale=x_planes[QUADRANT_BLOCKS * z : P, cols],
-                    start=(z == 0),
-                    stop=(z == PASSES - 1),
-                )
+        def multiply(tap, z, h):
+            cols = pieces[tap][h]
+            nc.tensor.matmul_mx(
+                out=acc[tap][h][:],
+                lhsT=w_code[z][:, tap * N : (tap + 1) * N].bitcast(FP8X4),
+                lhsT_scale=w_plane[z][:, tap * N : (tap + 1) * N],
+                rhs=x_code[z][:, cols].bitcast(FP8X4),
+                rhs_scale=x_planes[QUADRANT_BLOCKS * z : P, cols],
+                start=(z == 0),
+                stop=(z == PASSES - 1),
+            )
 
-        quantise_weight(1, 0, nc.vector.tensor_copy)
-        nc.vector.tensor_copy(x_planes[:], scale_table[:].indirect(offsets[:]))
-        gather_words(0)
-        multiply(1, 0)
-        quantise_weight(0, 0, nc.scalar.copy)
-        multiply(0, 0)
-        gather_words(1)
-        quantise_weight(1, 1, nc.scalar.copy)
-        quantise_weight(0, 1, nc.scalar.copy)
-        multiply(1, 1)
+        def shift_out(h, copy):
+            cols = pieces[1][h]
+            stop = min(cols.stop + 1, S)
+            copy(shifted[:, cols.start + 1 : stop], acc[1][h][:, 0 : stop - cols.start - 1])
 
-        nc.scalar.copy(shifted[:, 1 : HALF + 1], acc[1][0][:])
-        nc.scalar.copy(shifted[:, HALF + 1 : S], acc[1][1][:, 0 : HALF - 1])
-        multiply(0, 1)
-        for h, cols in enumerate(halves):
-            result = pool.tile([P, HALF], F32, name="result%d" % h, align_bytes=ALIGN)
-            nc.vector.tensor_tensor(result[:], acc[0][h][:], shifted[:, cols], mybir.AluOpType.add)
-            nc.sync.dma_start(out[:, cols], result[:])
+        result = pool.tile([P, S], F32, name="result", align_bytes=ALIGN)
+
+        def add_taps(h):
+            cols = pieces[0][h]
+            nc.vector.tensor_tensor(result[:, cols], acc[0][h][:], shifted[:, cols], mybir.AluOpType.add)
+
+        def store(cols, queue):
+            queue.dma_start(out[:, cols], result[:, cols])
+
+        whole = slice(0, S)
+        gather_words(0, whole)
+        gather_scales(whole)
+        round_weight(1, 0, nc.scalar.copy)
+        quantise(0, N, 2 * N)
+        multiply(1, 0, 0)
+        multiply(1, 0, 1)
+        multiply(1, 0, 2)
+        multiply(1, 0, 3)
+        round_weight(0, 0, nc.scalar.copy)
+        quantise(0, 0, N)
+        multiply(0, 0, 0)
+        multiply(0, 0, 1)
+        multiply(0, 0, 2)
+        multiply(0, 0, 3)
+        gather_words(1, whole)
+        round_weight(1, 1, nc.scalar.copy)
+        quantise(1, N, 2 * N)
+        round_weight(0, 1, nc.scalar.copy)
+        quantise(1, 0, N)
+        multiply(1, 1, 0)
+        multiply(1, 1, 1)
+        multiply(1, 1, 2)
+        multiply(1, 1, 3)
+        shift_out(0, nc.scalar.copy)
+        shift_out(1, nc.scalar.copy)
+        shift_out(2, nc.scalar.copy)
+        shift_out(3, nc.scalar.copy)
+        multiply(0, 1, 0)
+        multiply(0, 1, 1)
+        multiply(0, 1, 2)
+        multiply(0, 1, 3)
+        add_taps(0)
+        add_taps(1)
+        store(halves[0], nc.sync)
+        add_taps(2)
+        store(pieces[0][2], nc.sync)
+        add_taps(3)
+        store(pieces[0][3], nc.sync)

@@ -145,8 +145,9 @@ def tile_picked_listconv_none_p_kernel(tc, x_words, x_scales, w1, w2, offs, out)
         multiply(0, 0, 3)
         gather_words(1, whole)
         round_weight(1, 1, nc.scalar.copy)
+        round_weight(0, 1, nc.scalar.copy, 0, 64)
+        round_weight(0, 1, nc.vector.tensor_copy, 64, N)
         quantise(1, N, 2 * N)
-        round_weight(0, 1, nc.scalar.copy)
         quantise(1, 0, N)
         multiply(1, 1, 0)
         multiply(1, 1, 1)
@@ -161,9 +162,9 @@ def tile_picked_listconv_none_p_kernel(tc, x_words, x_scales, w1, w2, offs, out)
         multiply(0, 1, 2)
         multiply(0, 1, 3)
         add_taps(0)
+        store(pieces[0][0], nc.sync)
         add_taps(1)
-        store(halves[0], nc.sync)
+        store(pieces[0][1], nc.sync)
         add_taps(2)
-        store(pieces[0][2], nc.sync)
         add_taps(3)
-        store(pieces[0][3], nc.sync)
+        store(halves[1], nc.sync)

@@ -18,7 +18,7 @@ PASSES = K // K_PASS
 QUADRANT = 32
 QUADRANT_BLOCKS = 4
 LIST_GROUP = 16
-ALIGN = 64
+ALIGN = 256
 HALF = S // 2
 
 

@@ -12,6 +12,7 @@ U8 = mybir.dt.uint8
 FP8X4 = mybir.dt.float8_e4m3fn_x4
 
 P = 128
+TAPS = 2
 PACK = 4
 K_PASS = P * PACK
 PASSES = K // K_PASS
@@ -19,13 +20,18 @@ QUADRANT = 32
 QUADRANT_BLOCKS = 4
 LIST_GROUP = 16
 ALIGN = 256
-HALF = S // 2
+RUN = 4
+PIECE = 128
+PIECES = S // PIECE
+SHARE = N // 2
+EARLY = 3 * PIECE
+WARM = 2 * PIECE
 
 
 def tile_picked_listconv_none_p_kernel(tc, x_words, x_scales, w1, w2, offs, out):
     nc = tc.nc
     weights = (w1, w2)
-    halves = [slice(0, HALF), slice(HALF, S)]
+    pieces = [slice(h * PIECE, (h + 1) * PIECE) for h in range(PIECES)]
     with (
         tc.tile_pool(name="sbuf", bufs=1) as pool,
         tc.psum_pool(name="psum", bufs=1) as psum,
@@ -33,19 +39,20 @@ def tile_picked_listconv_none_p_kernel(tc, x_words, x_scales, w1, w2, offs, out)
         word_table = {}
         w_rows = {}
 
-        def load_words(z, queue):
+        def load_words(z):
             word_table[z] = pool.tile([P, T], I32, name="word_table%d" % z, align_bytes=ALIGN)
-            queue.dma_start(word_table[z][:], x_words[z].rearrange("p n t -> p (n t)").bitcast(I32))
+            nc.sync.dma_start(word_table[z][:], x_words[z].rearrange("p n t -> p (n t)").bitcast(I32))
 
-        def load_weight(tap, z, queue):
-            flat = pool.tile([P, PACK * N], F32, name="w_rows%d%d" % (tap, z), align_bytes=ALIGN)
+        def load_weight(tap, z):
+            label = "w_rows%d%d" % (tap, z)
+            flat = pool.tile([P, PACK * N], F32, name=label, tag=label, align_bytes=ALIGN)
             w_rows[tap, z] = flat[:].rearrange("p (t m) -> p t m", t=PACK)
             rows = weights[tap][z * K_PASS : (z + 1) * K_PASS, :]
-            queue.dma_start(flat[:], rows.rearrange("(p t) m -> p (t m)", t=PACK))
+            nc.sync.dma_start(flat[:], rows.rearrange("(p t) m -> p (t m)", t=PACK))
 
         offsets = pool.tile([P, S // LIST_GROUP], U16, name="offsets")
         nc.sync.dma_start(offsets[:], offs)
-        load_words(0, nc.sync)
+        load_words(0)
 
         scale_table = pool.tile([P, T], U8, name="scale_table", align_bytes=ALIGN)
         nc.vector.memset(scale_table[:].bitcast(I32), 0)
@@ -60,111 +67,108 @@ def tile_picked_listconv_none_p_kernel(tc, x_words, x_scales, w1, w2, offs, out)
         shifted = pool.tile([P, S], F32, name="shifted", align_bytes=ALIGN)
         nc.scalar.copy(shifted[:, 0:1], zero[:])
 
-        load_weight(1, 0, nc.sync)
-        load_weight(0, 0, nc.sync)
-        load_words(1, nc.sync)
-        load_weight(1, 1, nc.sync)
-        load_weight(0, 1, nc.sync)
+        load_weight(1, 0)
+        load_weight(0, 0)
+        load_words(1)
+        load_weight(1, 1)
+        load_weight(0, 1)
 
-        x_planes = pool.tile([P, S], U8, name="x_planes", align_bytes=ALIGN)
+        x_planes = {}
+        early_planes = pool.tile([P, EARLY], U8, name="x_planes", align_bytes=ALIGN)
         x_code = [pool.tile([P, S], U32, name="x_code%d" % z, align_bytes=ALIGN) for z in range(PASSES)]
 
-        def listed(cols):
-            return offsets[:, cols.start // LIST_GROUP : cols.stop // LIST_GROUP]
+        def gather_scales(entries, picked):
+            listed = offsets[:, entries.start // LIST_GROUP : entries.stop // LIST_GROUP]
+            nc.vector.tensor_copy(picked[:], scale_table[:].indirect(listed))
+            for first in range(entries.start, entries.stop, PIECE):
+                x_planes[first] = picked[:, first - entries.start : first - entries.start + PIECE]
 
-        def gather_scales(cols):
-            nc.vector.tensor_copy(x_planes[:, cols], scale_table[:].indirect(listed(cols)))
+        def gather_words(z):
+            nc.vector.tensor_copy(x_code[z][:], word_table[z][:].bitcast(U32).indirect(offsets[:]))
 
-        def gather_words(z, cols):
-            nc.vector.tensor_copy(x_code[z][:, cols], word_table[z][:].bitcast(U32).indirect(listed(cols)))
-
-        grouped = [pool.tile([P, 2 * N * PACK], BF16, name="grouped%d" % z, align_bytes=ALIGN) for z in range(PASSES)]
-        w_code = [pool.tile([P, 2 * N], U32, name="w_code%d" % z, align_bytes=ALIGN) for z in range(PASSES)]
-        w_plane = [pool.tile([P, 2 * N], U8, name="w_plane%d" % z, align_bytes=ALIGN) for z in range(PASSES)]
+        grouped = [pool.tile([P, TAPS * N * PACK], BF16, name="grouped%d" % z, align_bytes=ALIGN) for z in range(PASSES)]
+        w_code = [pool.tile([P, TAPS * N], U32, name="w_code%d" % z, align_bytes=ALIGN) for z in range(PASSES)]
+        w_plane = [pool.tile([P, TAPS * N], U8, name="w_plane%d" % z, align_bytes=ALIGN) for z in range(PASSES)]
 
         def round_weight(tap, z, copy, first=0, last=N):
             target = grouped[z][:, (tap * N + first) * PACK : (tap * N + last) * PACK]
             copy(
-                target.rearrange("p (c i t) -> p c t i", i=4, t=PACK),
-                w_rows[tap, z][:, :, first:last].rearrange("p t (c i) -> p c t i", i=4),
+                target.rearrange("p (c i t) -> p c t i", i=RUN, t=PACK),
+                w_rows[tap, z][:, :, first:last].rearrange("p t (c i) -> p c t i", i=RUN),
             )
 
-        def quantise(z, first, last):
+        def quantise(tap, z):
             nc.vector.quantize_mx(
-                out=w_code[z][:, first:last].bitcast(FP8X4),
-                scales=w_plane[z][:, first:last],
-                in_=grouped[z][:, first * PACK : last * PACK],
+                out=w_code[z][:, tap * N : (tap + 1) * N].bitcast(FP8X4),
+                scales=w_plane[z][:, tap * N : (tap + 1) * N],
+                in_=grouped[z][:, tap * N * PACK : (tap + 1) * N * PACK],
             )
 
-        pieces = [[slice(0, 128), slice(128, 256), slice(256, 384), slice(384, 512)], [slice(0, 128), slice(128, 256), slice(256, 384), slice(384, 512)]]
-        acc = [
-            [psum.tile([P, cols.stop - cols.start], F32, name="acc%d%d" % (tap, h)) for h, cols in enumerate(pieces[tap])]
-            for tap in range(2)
-        ]
+        banks = [[psum.tile([P, S], F32, name="acc%d%d" % (tap, h)) for h in range(PIECES)] for tap in range(TAPS)]
+        acc = [[bank[:, 0:PIECE] for bank in banks[tap]] for tap in range(TAPS)]
 
-        def multiply(tap, z, h):
-            cols = pieces[tap][h]
+        def warm_up():
             nc.tensor.matmul_mx(
-                out=acc[tap][h][:],
-                lhsT=w_code[z][:, tap * N : (tap + 1) * N].bitcast(FP8X4),
-                lhsT_scale=w_plane[z][:, tap * N : (tap + 1) * N],
-                rhs=x_code[z][:, cols].bitcast(FP8X4),
-                rhs_scale=x_planes[QUADRANT_BLOCKS * z : P, cols],
-                start=(z == 0),
-                stop=(z == PASSES - 1),
+                out=banks[0][PIECES - 1][:, 0:WARM],
+                lhsT=x_code[0][:, 0:N].bitcast(FP8X4),
+                lhsT_scale=early_planes[:, 0:N],
+                rhs=x_code[0][:, 0:WARM].bitcast(FP8X4),
+                rhs_scale=early_planes[:, 0:WARM],
+                start=True,
+                stop=True,
             )
 
-        def shift_out(h, copy):
-            cols = pieces[1][h]
-            stop = min(cols.stop + 1, S)
-            copy(shifted[:, cols.start + 1 : stop], acc[1][h][:, 0 : stop - cols.start - 1])
+        def multiply(tap, z):
+            for h, entries in enumerate(pieces):
+                nc.tensor.matmul_mx(
+                    out=acc[tap][h][:],
+                    lhsT=w_code[z][:, tap * N : (tap + 1) * N].bitcast(FP8X4),
+                    lhsT_scale=w_plane[z][:, tap * N : (tap + 1) * N],
+                    rhs=x_code[z][:, entries].bitcast(FP8X4),
+                    rhs_scale=x_planes[entries.start][QUADRANT_BLOCKS * z : P, :],
+                    start=(z == 0),
+                    stop=(z == PASSES - 1),
+                )
+
+        def shift_out(h):
+            first, stop = pieces[h].start + 1, min(pieces[h].stop + 1, S)
+            nc.scalar.copy(shifted[:, first:stop], acc[1][h][:, 0 : stop - first])
 
         result = pool.tile([P, S], F32, name="result", align_bytes=ALIGN)
 
         def add_taps(h):
-            cols = pieces[0][h]
-            nc.vector.tensor_tensor(result[:, cols], acc[0][h][:], shifted[:, cols], mybir.AluOpType.add)
+            entries = pieces[h]
+            nc.vector.tensor_tensor(result[:, entries], acc[0][h][:], shifted[:, entries], mybir.AluOpType.add)
 
-        def store(cols, queue):
-            queue.dma_start(out[:, cols], result[:, cols])
+        def store(entries):
+            nc.sync.dma_start(out[:, entries], result[:, entries])
 
-        whole = slice(0, S)
-        gather_words(0, whole)
-        gather_scales(whole)
+        gather_words(0)
+        gather_scales(slice(0, EARLY), early_planes)
+        warm_up()
         round_weight(1, 0, nc.scalar.copy)
-        quantise(0, N, 2 * N)
-        multiply(1, 0, 0)
-        multiply(1, 0, 1)
-        multiply(1, 0, 2)
-        multiply(1, 0, 3)
+        quantise(1, 0)
+        late_planes = pool.tile([P, S - EARLY], U8, name="late_planes", tag="w_rows10", align_bytes=ALIGN)
+        gather_scales(slice(EARLY, S), late_planes)
+        multiply(1, 0)
         round_weight(0, 0, nc.scalar.copy)
-        quantise(0, 0, N)
-        multiply(0, 0, 0)
-        multiply(0, 0, 1)
-        multiply(0, 0, 2)
-        multiply(0, 0, 3)
-        gather_words(1, whole)
+        quantise(0, 0)
+        multiply(0, 0)
+
+        gather_words(1)
         round_weight(1, 1, nc.scalar.copy)
-        round_weight(0, 1, nc.scalar.copy, 0, 64)
-        round_weight(0, 1, nc.vector.tensor_copy, 64, N)
-        quantise(1, N, 2 * N)
-        quantise(1, 0, N)
-        multiply(1, 1, 0)
-        multiply(1, 1, 1)
-        multiply(1, 1, 2)
-        multiply(1, 1, 3)
-        shift_out(0, nc.scalar.copy)
-        shift_out(1, nc.scalar.copy)
-        shift_out(2, nc.scalar.copy)
-        shift_out(3, nc.scalar.copy)
-        multiply(0, 1, 0)
-        multiply(0, 1, 1)
-        multiply(0, 1, 2)
-        multiply(0, 1, 3)
-        add_taps(0)
-        store(pieces[0][0], nc.sync)
-        add_taps(1)
-        store(pieces[0][1], nc.sync)
-        add_taps(2)
-        add_taps(3)
-        store(halves[1], nc.sync)
+        round_weight(0, 1, nc.scalar.copy, 0, SHARE)
+        round_weight(0, 1, nc.vector.tensor_copy, SHARE, N)
+        quantise(1, 1)
+        quantise(0, 1)
+        multiply(1, 1)
+        for h in range(PIECES):
+            shift_out(h)
+        multiply(0, 1)
+
+        for h in range(PIECES // 2):
+            add_taps(h)
+            store(pieces[h])
+        for h in range(PIECES // 2, PIECES):
+            add_taps(h)
+        store(slice(S // 2, S))

@@ -25,7 +25,6 @@ PIECE = 128
 PIECES = S // PIECE
 SHARE = N // 2
 EARLY = 3 * PIECE
-WARM = 2 * PIECE
 
 
 def tile_picked_listconv_none_p_kernel(tc, x_words, x_scales, w1, w2, offs, out):
@@ -107,17 +106,6 @@ def tile_picked_listconv_none_p_kernel(tc, x_words, x_scales, w1, w2, offs, out)
         banks = [[psum.tile([P, S], F32, name="acc%d%d" % (tap, h)) for h in range(PIECES)] for tap in range(TAPS)]
         acc = [[bank[:, 0:PIECE] for bank in banks[tap]] for tap in range(TAPS)]
 
-        def warm_up():
-            nc.tensor.matmul_mx(
-                out=banks[0][PIECES - 1][:, 0:WARM],
-                lhsT=x_code[0][:, 0:N].bitcast(FP8X4),
-                lhsT_scale=early_planes[:, 0:N],
-                rhs=x_code[0][:, 0:WARM].bitcast(FP8X4),
-                rhs_scale=early_planes[:, 0:WARM],
-                start=True,
-                stop=True,
-            )
-
         def multiply(tap, z):
             for h, entries in enumerate(pieces):
                 nc.tensor.matmul_mx(
@@ -145,7 +133,6 @@ def tile_picked_listconv_none_p_kernel(tc, x_words, x_scales, w1, w2, offs, out)
 
         gather_words(0)
         gather_scales(slice(0, EARLY), early_planes)
-        warm_up()
         round_weight(1, 0, nc.scalar.copy)
         quantise(1, 0)
         late_planes = pool.tile([P, S - EARLY], U8, name="late_planes", tag="w_rows10", align_bytes=ALIGN)

@@ -50,8 +50,8 @@ def tile_picked_listconv_none_p_kernel(tc, x_words, x_scales, w1, w2, offs, out)
             nc.sync.dma_start(flat[:], rows.rearrange("(p t) m -> p (t m)", t=PACK))
 
         offsets = pool.tile([P, S // LIST_GROUP], U16, name="offsets")
-        nc.sync.dma_start(offsets[:], offs)
         load_words(0)
+        nc.sync.dma_start(offsets[:], offs)
 
         scale_table = pool.tile([P, T], U8, name="scale_table", align_bytes=ALIGN)
         nc.vector.memset(scale_table[:].bitcast(I32), 0)

import concourse.mybir as mybir

K, T, S, N = 1024, 1024, 512, 128
FLOPS = 2 * 2 * K * N * S

F32 = mybir.dt.float32
BF16 = mybir.dt.bfloat16
I32 = mybir.dt.int32
U32 = mybir.dt.uint32
U16 = mybir.dt.uint16
U8 = mybir.dt.uint8
FP8X4 = mybir.dt.float8_e4m3fn_x4

P = 128
TAPS = 2
PACK = 4
K_PASS = P * PACK
PASSES = K // K_PASS
QUADRANT = 32
QUADRANT_BLOCKS = 4
LIST_GROUP = 16
ALIGN = 256
RUN = 4
PIECE = 128
PIECES = S // PIECE
SHARE = N // 2
EARLY = 3 * PIECE


def tile_picked_listconv_none_p_kernel(tc, x_words, x_scales, w1, w2, offs, out):
    nc = tc.nc
    weights = (w1, w2)
    pieces = [slice(h * PIECE, (h + 1) * PIECE) for h in range(PIECES)]
    with (
        tc.tile_pool(name="sbuf", bufs=1) as pool,
        tc.psum_pool(name="psum", bufs=1) as psum,
    ):
        word_table = {}
        w_rows = {}

        def load_words(z):
            word_table[z] = pool.tile([P, T], I32, name="word_table%d" % z, align_bytes=ALIGN)
            nc.sync.dma_start(word_table[z][:], x_words[z].rearrange("p n t -> p (n t)").bitcast(I32))

        def load_weight(tap, z):
            label = "w_rows%d%d" % (tap, z)
            flat = pool.tile([P, PACK * N], F32, name=label, tag=label, align_bytes=ALIGN)
            w_rows[tap, z] = flat[:].rearrange("p (t m) -> p t m", t=PACK)
            rows = weights[tap][z * K_PASS : (z + 1) * K_PASS, :]
            nc.sync.dma_start(flat[:], rows.rearrange("(p t) m -> p (t m)", t=PACK))

        offsets = pool.tile([P, S // LIST_GROUP], U16, name="offsets")
        load_words(0)
        nc.sync.dma_start(offsets[:], offs)

        scale_table = pool.tile([P, T], U8, name="scale_table", align_bytes=ALIGN)
        nc.vector.memset(scale_table[:].bitcast(I32), 0)
        for q in range(P // QUADRANT):
            nc.sync.dma_start(
                scale_table[QUADRANT * q : QUADRANT * q + PASSES * QUADRANT_BLOCKS, :].bitcast(I32),
                x_scales[:, QUADRANT_BLOCKS * q : QUADRANT_BLOCKS * (q + 1), :].bitcast(I32),
            )

        zero = pool.tile([P, 1], F32, name="zero", align_bytes=ALIGN)
        nc.vector.memset(zero[:], 0.0)
        shifted = pool.tile([P, S], F32, name="shifted", align_bytes=ALIGN)
        nc.scalar.copy(shifted[:, 0:1], zero[:])

        load_weight(1, 0)
        load_weight(0, 0)
        load_words(1)
        load_weight(1, 1)
        load_weight(0, 1)

        x_planes = {}
        early_planes = pool.tile([P, EARLY], U8, name="x_planes", align_bytes=ALIGN)
        x_code = [pool.tile([P, S], U32, name="x_code%d" % z, align_bytes=ALIGN) for z in range(PASSES)]

        def gather_scales(entries, picked):
            listed = offsets[:, entries.start // LIST_GROUP : entries.stop // LIST_GROUP]
            nc.vector.tensor_copy(picked[:], scale_table[:].indirect(listed))
            for first in range(entries.start, entries.stop, PIECE):
                x_planes[first] = picked[:, first - entries.start : first - entries.start + PIECE]

        def gather_words(z):
            nc.vector.tensor_copy(x_code[z][:], word_table[z][:].bitcast(U32).indirect(offsets[:]))

        grouped = [pool.tile([P, TAPS * N * PACK], BF16, name="grouped%d" % z, align_bytes=ALIGN) for z in range(PASSES)]
        w_code = [pool.tile([P, TAPS * N], U32, name="w_code%d" % z, align_bytes=ALIGN) for z in range(PASSES)]
        w_plane = [pool.tile([P, TAPS * N], U8, name="w_plane%d" % z, align_bytes=ALIGN) for z in range(PASSES)]

        def round_weight(tap, z, copy, first=0, last=N):
            target = grouped[z][:, (tap * N + first) * PACK : (tap * N + last) * PACK]
            copy(
                target.rearrange("p (c i t) -> p c t i", i=RUN, t=PACK),
                w_rows[tap, z][:, :, first:last].rearrange("p t (c i) -> p c t i", i=RUN),
            )

        def quantise(tap, z):
            nc.vector.quantize_mx(
                out=w_code[z][:, tap * N : (tap + 1) * N].bitcast(FP8X4),
                scales=w_plane[z][:, tap * N : (tap + 1) * N],
                in_=grouped[z][:, tap * N * PACK : (tap + 1) * N * PACK],
            )

        banks = [[psum.tile([P, S], F32, name="acc%d%d" % (tap, h)) for h in range(PIECES)] for tap in range(TAPS)]
        acc = [[bank[:, 0:PIECE] for bank in banks[tap]] for tap in range(TAPS)]

        def multiply(tap, z):
            for h, entries in enumerate(pieces):
                nc.tensor.matmul_mx(
                    out=acc[tap][h][:],
                    lhsT=w_code[z][:, tap * N : (tap + 1) * N].bitcast(FP8X4),
                    lhsT_scale=w_plane[z][:, tap * N : (tap + 1) * N],
                    rhs=x_code[z][:, entries].bitcast(FP8X4),
                    rhs_scale=x_planes[entries.start][QUADRANT_BLOCKS * z : P, :],
                    start=(z == 0),
                    stop=(z == PASSES - 1),
                )

        def shift_out(h):
            first, stop = pieces[h].start + 1, min(pieces[h].stop + 1, S)
            nc.scalar.copy(shifted[:, first:stop], acc[1][h][:, 0 : stop - first])

        result = pool.tile([P, S], F32, name="result", align_bytes=ALIGN)

        def add_taps(h):
            entries = pieces[h]
            nc.vector.tensor_tensor(result[:, entries], acc[0][h][:], shifted[:, entries], mybir.AluOpType.add)

        def store(entries):
            nc.sync.dma_start(out[:, entries], result[:, entries])

        gather_words(0)
        gather_scales(slice(0, EARLY), early_planes)
        round_weight(1, 0, nc.scalar.copy)
        quantise(1, 0)
        late_planes = pool.tile([P, S - EARLY], U8, name="late_planes", tag="w_rows10", align_bytes=ALIGN)
        gather_scales(slice(EARLY, S), late_planes)
        multiply(1, 0)
        round_weight(0, 0, nc.scalar.copy)
        quantise(0, 0)
        multiply(0, 0)

        gather_words(1)
        round_weight(1, 1, nc.scalar.copy)
        round_weight(0, 1, nc.scalar.copy, 0, SHARE)
        round_weight(0, 1, nc.vector.tensor_copy, SHARE, N)
        quantise(1, 1)
        quantise(0, 1)
        multiply(1, 1)
        for h in range(PIECES):
            shift_out(h)
        multiply(0, 1)

        for h in range(PIECES // 2):
            add_taps(h)
            store(pieces[h])
        for h in range(PIECES // 2, PIECES):
            add_taps(h)
        store(slice(S // 2, S))
